import numpy as np
import ml_dtypes


def mxq(x, axis, fmt="e4m3"):
    dtype, down = {"e4m3": (ml_dtypes.float8_e4m3fn, 7), "e5m2": (ml_dtypes.float8_e5m2, 14)}[fmt]
    v = np.moveaxis(np.asarray(x, np.float32).astype(ml_dtypes.bfloat16).astype(np.float64), axis, -1)
    blocks = v.reshape(v.shape[:-1] + (-1, 32))
    amax = np.abs(blocks).max(-1, keepdims=True)
    byte = np.maximum(np.where(amax > 0, np.frexp(amax)[1] - 1 + 127, 0) - down, 1)
    scale = np.exp2(byte - 127.0)
    codes = (blocks / scale).astype(np.float32).astype(dtype).astype(np.float64)
    return np.moveaxis((codes * scale).reshape(v.shape), -1, axis)


WIDE = False


def mx_kscale(k):
    if not WIDE:
        return np.ones(k)
    levels = np.array([30, -30])
    if k % 512:
        return np.exp2(np.random.permutation(np.resize(levels, k // 32))).repeat(32)
    a = np.empty((k // 512, 16))
    for p in range(k // 512):
        a[p, :8] = np.random.permutation(np.resize(levels, 8))
        for g in range(8):
            far = levels[np.abs(levels - a[p, g]) >= 10]
            a[p, g + 8] = far[np.random.randint(len(far))]
    return np.exp2(a.ravel()).repeat(32)


def f64(x):
    return np.asarray(x).astype(np.float64)


def striped(idx):
    return np.tile(np.asarray(idx).reshape(-1, 16).T, (8, 1)).astype(np.uint16)


def unstriped(offs):
    return offs[:16].T.reshape(-1).astype(np.int64)


def bf(x):
    return np.asarray(x, np.float32).astype(ml_dtypes.bfloat16)


def planes(Y):
    r, m = Y.shape
    b = f64(bf(Y)).reshape(r // 32, 32, m)
    amax = np.abs(b).max(1)
    byte = np.clip(np.where(amax > 0, np.frexp(amax)[1] - 1 + 127 - 7, 1), 1, 254)
    codes = (b * np.exp2(127.0 - byte)[:, None, :]).reshape(r, m).astype(np.float32).astype(ml_dtypes.float8_e4m3fn).view(np.uint8)
    words = codes.reshape(r // 512, 128, 4, m).transpose(0, 1, 3, 2)
    return np.ascontiguousarray(words), np.ascontiguousarray(byte.astype(np.uint8).reshape(r // 512, 16, m))


K, N, T, J = 512, 512, 2048, 512


def setup_inputs():
    n = np.random.standard_normal
    idx = np.random.permutation(T)[:J]
    fj = mx_kscale(J)
    tj = np.ones(T)
    tj[idx] = fj
    return {
        "xt": (n((K, T)) * tj).astype(np.float32),
        "g": (n((N, T)) * np.exp(0.5 * n((1, T))) / tj).astype(np.float32),
        "mom": (0.5 * n((K, N))).astype(np.float32),
        "offs": striped(idx),
    }


def reference(xt, g, mom, offs):
    idx = unstriped(offs)
    xj = f64(xt)[:, idx].T
    gj = f64(g)[:, idx].T
    xjq = mxq(xj, 0, "e4m3")
    gjq = mxq(gj, 0, "e5m2")
    w = xjq.T @ gjq
    y = 0.04 * w + 0.9 * f64(mom)
    words, scales = planes(y)
    return y, words, scales

@@ -1,0 +1,149 @@
+from contextlib import ExitStack
+
+import concourse.mybir as mybir
+from concourse.masks import make_identity
+
+K, N, T, J = 512, 512, 2048, 512
+FLOPS = 2 * K * N * J
+
+F32 = mybir.dt.float32
+BF16 = mybir.dt.bfloat16
+I32 = mybir.dt.int32
+U32 = mybir.dt.uint32
+U16 = mybir.dt.uint16
+U8 = mybir.dt.uint8
+E4M3 = mybir.dt.float8_e4m3fn_x4
+E5M2 = mybir.dt.float8_e5m2_x4
+MULT = mybir.AluOpType.mult
+ADD = mybir.AluOpType.add
+COPY = mybir.ActivationFunctionType.Copy
+
+P = 128
+PACK = 4
+HALF = N // 2
+
+
+def tile_list_wgrad_listed_pl_kernel(tc, xt, g, mom, offs, out_0, out_1, out_2):
+    nc = tc.nc
+    with ExitStack() as ctx:
+        keep = ctx.enter_context(tc.tile_pool(name="keep", bufs=1))
+        turn = ctx.enter_context(tc.psum_pool(name="turn", bufs=2))
+        sums = ctx.enter_context(tc.psum_pool(name="sums", bufs=1))
+
+        x_rows = xt.rearrange("(p t) c -> t p c", t=PACK)
+        mom_rows = mom.rearrange("(p t) n -> p (t n)", t=PACK)
+        y_rows = out_0.rearrange("(p t) n -> p (t n)", t=PACK)
+        words_out = out_1.rearrange("z p c r -> p (z c r)").bitcast(I32)
+        scales_out = out_2.rearrange("z q c -> (z q) c").bitcast(I32)
+
+        offsets = keep.tile([P, J // 16], U16, name="offsets")
+        g_win = [keep.tile([P, T], F32, name=f"g_win{c}") for c in range(4)]
+        x_win = [keep.tile([P, T], F32, name=f"x_win{t}", tag=f"x_win{t}", align_bytes=64) for t in range(PACK)]
+        mom01 = keep.tile([P, 2 * N], F32, name="mom01", tag="mom01", align_bytes=64)
+        mom23 = keep.tile([P, 2 * N], F32, name="mom23")
+
+        nc.sync.dma_start(g_win[0][:], g[0:P, :])
+        nc.sync.dma_start(offsets[:], offs)
+        for c in range(1, 4):
+            nc.sync.dma_start(g_win[c][:], g[c * P : (c + 1) * P, :])
+        for t in range(PACK):
+            nc.sync.dma_start(x_win[t][:], x_rows[t])
+        nc.sync.dma_start(mom01[:], mom_rows[:, 0 : 2 * N])
+        nc.sync.dma_start(mom23[:], mom_rows[:, 2 * N : 4 * N])
+
+        ident = keep.tile([P, P], F32, name="ident")
+        make_identity(nc, ident[:])
+
+        def listed_rows(window, grouped, label):
+            picked = keep.tile([P, J], BF16, name=f"picked_{label}", tag=f"picked_{label}", align_bytes=64)
+            nc.vector.tensor_copy(picked[:], window[:].indirect(offsets[:]))
+            pairs = picked[:].bitcast(F32)
+            turned = turn.tile([P, 2, P], F32, name="turned")
+            for u in range(2):
+                nc.tensor.transpose(turned[:, u, :], pairs[:, u : J // 2 : 2], ident[:])
+            nc.scalar.copy(
+                grouped.bitcast(F32).rearrange("p (r u) -> p r u", u=2),
+                turned[:].rearrange("p u r -> p r u"),
+            )
+
+        g_grouped = keep.tile([P, N * PACK], BF16, name="g_grouped", align_bytes=64)
+        for c in range(4):
+            listed_rows(g_win[c], g_grouped[:, c * P * PACK : (c + 1) * P * PACK], f"g{c}")
+
+        def regroup(t):
+            x_grouped = keep.tile([P, P * PACK], BF16, name=f"x_grouped{t}", tag=f"x_grouped{t}", align_bytes=64)
+            listed_rows(x_win[t], x_grouped[:], f"x{t}")
+            return x_grouped
+
+        def product(t, x_grouped, codes_tag):
+            x_codes = keep.tile([P, P], U32, name=f"x_codes{t}", tag=codes_tag, align_bytes=64)
+            x_scales = keep.tile([P, P], U8, name=f"x_scales{t}", align_bytes=64)
+            nc.vector.quantize_mx(out=x_codes[:].bitcast(E4M3), scales=x_scales[:], in_=x_grouped[:])
+            w = sums.tile([P, N], F32, name=f"w{t}")
+            nc.tensor.matmul_mx(
+                out=w[:],
+                lhsT=x_codes[:].bitcast(E4M3),
+                lhsT_scale=x_scales[:],
+                rhs=g_codes[:].bitcast(E5M2),
+                rhs_scale=g_scales[:],
+                start=True,
+                stop=True,
+            )
+            return w
+
+        def combine(y, w, kept):
+            nc.vector.scalar_tensor_tensor(out=y, in0=w, scalar=0.04, in1=kept, op0=MULT, op1=ADD)
+
+        halves = [slice(h * HALF, (h + 1) * HALF) for h in range(2)]
+
+        grouped = [regroup(0)]
+        g_codes = keep.tile([P, N], U32, name="g_codes", tag="x_win0", align_bytes=64)
+        g_scales = keep.tile([P, N], U8, name="g_scales", align_bytes=64)
+        nc.vector.quantize_mx(out=g_codes[:].bitcast(E5M2), scales=g_scales[:], in_=g_grouped[:])
+
+        step01 = keep.tile([P, 2 * N], F32, name="step01")
+        for t in range(2):
+            grouped.append(regroup(t + 1))
+            w = product(t, grouped[t], f"x_win{t + 1}")
+            nc.scalar.activation(step01[:, t * N : (t + 1) * N], w[:], COPY, scale=0.04)
+        grouped.append(regroup(3))
+        w2 = product(2, grouped[2], "x_win3")
+
+        y01 = keep.tile([P, 2 * N], F32, name="y01")
+        nc.vector.scalar_tensor_tensor(out=y01[:], in0=mom01[:], scalar=0.9, in1=step01[:], op0=MULT, op1=ADD)
+        nc.sync.dma_start(y_rows[:, 0 : 2 * N], y01[:])
+        w3 = product(3, grouped[3], "mom01")
+
+        y_bf = keep.tile([P, N * PACK], BF16, name="y_bf", align_bytes=64)
+        y_bf_half = [y_bf[:, h * HALF * PACK : (h + 1) * HALF * PACK] for h in range(2)]
+        y_bf_nt = [half.rearrange("p (n t) -> p n t", t=PACK) for half in y_bf_half]
+        y01_nt = y01[:].rearrange("p (t n) -> p n t", t=2)
+        for h in range(2):
+            nc.scalar.copy(y_bf_nt[h][:, :, 0:2], y01_nt[:, halves[h], :])
+
+        kept23 = keep.tile([P, 2 * N], F32, name="kept23", tag="x_grouped3", align_bytes=64)
+        nc.vector.tensor_scalar(out=kept23[:], in0=mom23[:], scalar1=0.9, scalar2=None, op0=MULT)
+
+        y23 = keep.tile([P, 2 * N], F32, name="y23")
+        for t, w in ((2, w2), (3, w3)):
+            for h in range(2):
+                first = (2 * h + t - 2) * HALF
+                kept_first = (t - 2) * N + h * HALF
+                combine(y23[:, first : first + HALF], w[:, halves[h]], kept23[:, kept_first : kept_first + HALF])
+                nc.sync.dma_start(y_rows[:, t * N + h * HALF : t * N + (h + 1) * HALF], y23[:, first : first + HALF])
+        y23_nt = [y23[:, h * N : (h + 1) * N].rearrange("p (t n) -> p n t", t=2) for h in range(2)]
+
+        y_codes = [keep.tile([P, HALF], U32, name=f"y_codes{h}", align_bytes=64) for h in range(2)]
+        y_scales = keep.tile([P, N], U8, name="y_scales", align_bytes=64)
+        nc.vector.tensor_copy(y_bf_nt[0][:, :, 2:4], y23_nt[0])
+        nc.scalar.copy(y_bf_nt[1][:, :, 2:4], y23_nt[1])
+        for h in range(2):
+            nc.vector.quantize_mx(
+                out=y_codes[h][:].bitcast(E4M3),
+                scales=y_scales[:, halves[h]],
+                in_=y_bf_half[h],
+            )
+            nc.sync.dma_start(words_out[:, halves[h]], y_codes[h][:].bitcast(I32))
+        for q in range(4):
+            queue = nc.scalar if q < 2 else nc.sync
+            queue.dma_start(scales_out[4 * q : 4 * q + 4, :], y_scales[32 * q : 32 * q + 4, :].bitcast(I32))

@@ -21,6 +21,7 @@ COPY = mybir.ActivationFunctionType.Copy
 P = 128
 PACK = 4
 HALF = N // 2
+SHARE = 192
 
 
 def tile_list_wgrad_listed_pl_kernel(tc, xt, g, mom, offs, out_0, out_1, out_2):
@@ -30,49 +31,54 @@ def tile_list_wgrad_listed_pl_kernel(tc, xt, g, mom, offs, out_0, out_1, out_2):
         turn = ctx.enter_context(tc.psum_pool(name="turn", bufs=2))
         sums = ctx.enter_context(tc.psum_pool(name="sums", bufs=1))
 
-        x_rows = xt.rearrange("(p t) c -> t p c", t=PACK)
+        x_rows = xt.rearrange("(p t) c -> p (t c)", t=PACK)
         mom_rows = mom.rearrange("(p t) n -> p (t n)", t=PACK)
         y_rows = out_0.rearrange("(p t) n -> p (t n)", t=PACK)
         words_out = out_1.rearrange("z p c r -> p (z c r)").bitcast(I32)
         scales_out = out_2.rearrange("z q c -> (z q) c").bitcast(I32)
 
         offsets = keep.tile([P, J // 16], U16, name="offsets")
-        g_win = [keep.tile([P, T], F32, name=f"g_win{c}") for c in range(4)]
+        g_win = [keep.tile([P, 2 * T], F32, name=f"g_win{c}") for c in range(2)]
         x_win = [keep.tile([P, T], F32, name=f"x_win{t}", tag=f"x_win{t}", align_bytes=64) for t in range(PACK)]
-        mom01 = keep.tile([P, 2 * N], F32, name="mom01", tag="mom01", align_bytes=64)
+        mom01 = keep.tile([P, 2 * N], F32, name="mom01")
         mom23 = keep.tile([P, 2 * N], F32, name="mom23")
 
-        nc.sync.dma_start(g_win[0][:], g[0:P, :])
+        g_rows = g.rearrange("(c p e) t -> c p (e t)", c=2, e=2)
+        nc.sync.dma_start(g_win[0][:], g_rows[0])
         nc.sync.dma_start(offsets[:], offs)
-        for c in range(1, 4):
-            nc.sync.dma_start(g_win[c][:], g[c * P : (c + 1) * P, :])
+        nc.sync.dma_start(g_win[1][:], g_rows[1])
         for t in range(PACK):
-            nc.sync.dma_start(x_win[t][:], x_rows[t])
+            nc.sync.dma_start(x_win[t][:], x_rows[:, t * T : (t + 1) * T])
         nc.sync.dma_start(mom01[:], mom_rows[:, 0 : 2 * N])
         nc.sync.dma_start(mom23[:], mom_rows[:, 2 * N : 4 * N])
 
         ident = keep.tile([P, P], F32, name="ident")
         make_identity(nc, ident[:])
 
-        def listed_rows(window, grouped, label):
-            picked = keep.tile([P, J], BF16, name=f"picked_{label}", tag=f"picked_{label}", align_bytes=64)
-            nc.vector.tensor_copy(picked[:], window[:].indirect(offsets[:]))
-            pairs = picked[:].bitcast(F32)
-            turned = turn.tile([P, 2, P], F32, name="turned")
-            for u in range(2):
-                nc.tensor.transpose(turned[:, u, :], pairs[:, u : J // 2 : 2], ident[:])
+        def listed_rows(windows, grouped, label):
+            rows = len(windows)
+            turned = turn.tile([P, rows, 2, P], F32, name="turned", tag="turned")
+            for e, window in enumerate(windows):
+                picked = keep.tile([P, J], BF16, name=f"picked_{label}_{e}", align_bytes=64)
+                nc.vector.tensor_copy(
+                    picked[:].rearrange("p (h b i) -> p b h i", h=2, i=16), window.indirect(offsets[:])
+                )
+                pairs = picked[:].bitcast(F32)
+                for u in range(2):
+                    nc.tensor.transpose(turned[:, e, u, :], pairs[:, u * P : (u + 1) * P], ident[:])
             nc.scalar.copy(
-                grouped.bitcast(F32).rearrange("p (r u) -> p r u", u=2),
-                turned[:].rearrange("p u r -> p r u"),
+                grouped.bitcast(F32).rearrange("p (r e u) -> p r e u", e=rows, u=2),
+                turned[:].rearrange("p e u r -> p r e u"),
             )
 
         g_grouped = keep.tile([P, N * PACK], BF16, name="g_grouped", align_bytes=64)
-        for c in range(4):
-            listed_rows(g_win[c], g_grouped[:, c * P * PACK : (c + 1) * P * PACK], f"g{c}")
+        for c in range(2):
+            windows = [g_win[c][:, e * T : (e + 1) * T] for e in range(2)]
+            listed_rows(windows, g_grouped[:, c * HALF * PACK : (c + 1) * HALF * PACK], f"g{c}")
 
         def regroup(t):
             x_grouped = keep.tile([P, P * PACK], BF16, name=f"x_grouped{t}", tag=f"x_grouped{t}", align_bytes=64)
-            listed_rows(x_win[t], x_grouped[:], f"x{t}")
+            listed_rows([x_win[t][:]], x_grouped[:], f"x{t}")
             return x_grouped
 
         def product(t, x_grouped, codes_tag):
@@ -101,47 +107,52 @@ def tile_list_wgrad_listed_pl_kernel(tc, xt, g, mom, offs, out_0, out_1, out_2):
         g_scales = keep.tile([P, N], U8, name="g_scales", align_bytes=64)
         nc.vector.quantize_mx(out=g_codes[:].bitcast(E5M2), scales=g_scales[:], in_=g_grouped[:])
 
-        step01 = keep.tile([P, 2 * N], F32, name="step01")
+        step = [keep.tile([P, N], F32, name=f"step{t}", tag=f"step{t}", align_bytes=64) for t in range(2)]
         for t in range(2):
             grouped.append(regroup(t + 1))
             w = product(t, grouped[t], f"x_win{t + 1}")
-            nc.scalar.activation(step01[:, t * N : (t + 1) * N], w[:], COPY, scale=0.04)
+            nc.scalar.activation(step[t][:], w[:], COPY, scale=0.04)
         grouped.append(regroup(3))
         w2 = product(2, grouped[2], "x_win3")
 
         y01 = keep.tile([P, 2 * N], F32, name="y01")
-        nc.vector.scalar_tensor_tensor(out=y01[:], in0=mom01[:], scalar=0.9, in1=step01[:], op0=MULT, op1=ADD)
+        for t in range(2):
+            cols = slice(t * N, (t + 1) * N)
+            nc.vector.scalar_tensor_tensor(
+                out=y01[:, cols], in0=mom01[:, cols], scalar=0.9, in1=step[t][:], op0=MULT, op1=ADD
+            )
         nc.sync.dma_start(y_rows[:, 0 : 2 * N], y01[:])
-        w3 = product(3, grouped[3], "mom01")
+        w3 = product(3, grouped[3], "step0")
 
-        y_bf = keep.tile([P, N * PACK], BF16, name="y_bf", align_bytes=64)
-        y_bf_half = [y_bf[:, h * HALF * PACK : (h + 1) * HALF * PACK] for h in range(2)]
-        y_bf_nt = [half.rearrange("p (n t) -> p n t", t=PACK) for half in y_bf_half]
+        kept23 = keep.tile([P, 2 * N], F32, name="kept23")
+        for t in range(2):
+            cols = slice(t * N, (t + 1) * N)
+            nc.scalar.activation(kept23[:, cols], mom23[:, cols], COPY, scale=0.9)
+
+        y_bf = keep.tile([P, N, PACK], BF16, name="y_bf", tag="x_grouped3", align_bytes=64)
         y01_nt = y01[:].rearrange("p (t n) -> p n t", t=2)
-        for h in range(2):
-            nc.scalar.copy(y_bf_nt[h][:, :, 0:2], y01_nt[:, halves[h], :])
-
-        kept23 = keep.tile([P, 2 * N], F32, name="kept23", tag="x_grouped3", align_bytes=64)
-        nc.vector.tensor_scalar(out=kept23[:], in0=mom23[:], scalar1=0.9, scalar2=None, op0=MULT)
+        nc.scalar.copy(y_bf[:, 0:SHARE, 0:2], y01_nt[:, 0:SHARE, :])
+        nc.vector.tensor_copy(y_bf[:, SHARE:N, 0:2], y01_nt[:, SHARE:N, :])
 
         y23 = keep.tile([P, 2 * N], F32, name="y23")
-        for t, w in ((2, w2), (3, w3)):
-            for h in range(2):
-                first = (2 * h + t - 2) * HALF
-                kept_first = (t - 2) * N + h * HALF
-                combine(y23[:, first : first + HALF], w[:, halves[h]], kept23[:, kept_first : kept_first + HALF])
-                nc.sync.dma_start(y_rows[:, t * N + h * HALF : t * N + (h + 1) * HALF], y23[:, first : first + HALF])
-        y23_nt = [y23[:, h * N : (h + 1) * N].rearrange("p (t n) -> p n t", t=2) for h in range(2)]
+        combine(y23[:, 0:N], w2[:], kept23[:, 0:N])
+        nc.sync.dma_start(y_rows[:, 2 * N : 3 * N], y23[:, 0:N])
+        for a, b in ((0, SHARE), (HALF, N), (SHARE, HALF)):
+            combine(y23[:, N + a : N + b], w3[:, a:b], kept23[:, N + a : N + b])
+        nc.sync.dma_start(y_rows[:, 3 * N : 4 * N], y23[:, N : 2 * N])
+
+        y23_nt = y23[:].rearrange("p (t n) -> p n t", t=2)
+        nc.scalar.copy(y_bf[:, 0:SHARE, 2:4], y23_nt[:, 0:SHARE, :])
+        nc.vector.tensor_copy(y_bf[:, HALF:N, 2:4], y23_nt[:, HALF:N, :])
+        nc.vector.tensor_copy(y_bf[:, SHARE:HALF, 2:4], y23_nt[:, SHARE:HALF, :])
 
         y_codes = [keep.tile([P, HALF], U32, name=f"y_codes{h}", align_bytes=64) for h in range(2)]
         y_scales = keep.tile([P, N], U8, name="y_scales", align_bytes=64)
-        nc.vector.tensor_copy(y_bf_nt[0][:, :, 2:4], y23_nt[0])
-        nc.scalar.copy(y_bf_nt[1][:, :, 2:4], y23_nt[1])
-        for h in range(2):
+        for h in (1, 0):
             nc.vector.quantize_mx(
                 out=y_codes[h][:].bitcast(E4M3),
                 scales=y_scales[:, halves[h]],
-                in_=y_bf_half[h],
+                in_=y_bf[:, halves[h], :].rearrange("p n t -> p (n t)"),
             )
             nc.sync.dma_start(words_out[:, halves[h]], y_codes[h][:].bitcast(I32))
         for q in range(4):

@@ -21,7 +21,7 @@ COPY = mybir.ActivationFunctionType.Copy
 P = 128
 PACK = 4
 HALF = N // 2
-SHARE = 192
+QUARTER = N // 4
 
 
 def tile_list_wgrad_listed_pl_kernel(tc, xt, g, mom, offs, out_0, out_1, out_2):
@@ -100,8 +100,6 @@ def tile_list_wgrad_listed_pl_kernel(tc, xt, g, mom, offs, out_0, out_1, out_2):
         def combine(y, w, kept):
             nc.vector.scalar_tensor_tensor(out=y, in0=w, scalar=0.04, in1=kept, op0=MULT, op1=ADD)
 
-        halves = [slice(h * HALF, (h + 1) * HALF) for h in range(2)]
-
         grouped = [regroup(0)]
         g_codes = keep.tile([P, N], U32, name="g_codes", tag="x_win0", align_bytes=64)
         g_scales = keep.tile([P, N], U8, name="g_scales", align_bytes=64)
@@ -129,32 +127,42 @@ def tile_list_wgrad_listed_pl_kernel(tc, xt, g, mom, offs, out_0, out_1, out_2):
             cols = slice(t * N, (t + 1) * N)
             nc.scalar.activation(kept23[:, cols], mom23[:, cols], COPY, scale=0.9)
 
-        y_bf = keep.tile([P, N, PACK], BF16, name="y_bf", tag="x_grouped3", align_bytes=64)
+        y_bf = [
+            keep.tile([P, HALF, PACK], BF16, name="y_bf0", tag="x_grouped3", align_bytes=64),
+            keep.tile([P, HALF, PACK], BF16, name="y_bf1", align_bytes=64),
+        ]
         y01_nt = y01[:].rearrange("p (t n) -> p n t", t=2)
-        nc.scalar.copy(y_bf[:, 0:SHARE, 0:2], y01_nt[:, 0:SHARE, :])
-        nc.vector.tensor_copy(y_bf[:, SHARE:N, 0:2], y01_nt[:, SHARE:N, :])
+        nc.scalar.copy(y_bf[0][:, :, 0:2], y01_nt[:, 0:HALF, :])
+        nc.vector.tensor_copy(y_bf[1][:, :, 0:2], y01_nt[:, HALF:N, :])
 
         y23 = keep.tile([P, 2 * N], F32, name="y23")
         combine(y23[:, 0:N], w2[:], kept23[:, 0:N])
         nc.sync.dma_start(y_rows[:, 2 * N : 3 * N], y23[:, 0:N])
-        for a, b in ((0, SHARE), (HALF, N), (SHARE, HALF)):
+        quarters = [(HALF, HALF + QUARTER), (HALF + QUARTER, N)]
+        for a, b in [(0, HALF)] + quarters:
             combine(y23[:, N + a : N + b], w3[:, a:b], kept23[:, N + a : N + b])
         nc.sync.dma_start(y_rows[:, 3 * N : 4 * N], y23[:, N : 2 * N])
 
         y23_nt = y23[:].rearrange("p (t n) -> p n t", t=2)
-        nc.scalar.copy(y_bf[:, 0:SHARE, 2:4], y23_nt[:, 0:SHARE, :])
-        nc.vector.tensor_copy(y_bf[:, HALF:N, 2:4], y23_nt[:, HALF:N, :])
-        nc.vector.tensor_copy(y_bf[:, SHARE:HALF, 2:4], y23_nt[:, SHARE:HALF, :])
+        nc.scalar.copy(y_bf[0][:, :, 2:4], y23_nt[:, 0:HALF, :])
+        for a, b in quarters:
+            nc.vector.tensor_copy(y_bf[1][:, a - HALF : b - HALF, 2:4], y23_nt[:, a:b, :])
 
         y_codes = [keep.tile([P, HALF], U32, name=f"y_codes{h}", align_bytes=64) for h in range(2)]
         y_scales = keep.tile([P, N], U8, name="y_scales", align_bytes=64)
-        for h in (1, 0):
+        for a, b in quarters:
             nc.vector.quantize_mx(
-                out=y_codes[h][:].bitcast(E4M3),
-                scales=y_scales[:, halves[h]],
-                in_=y_bf[:, halves[h], :].rearrange("p n t -> p (n t)"),
+                out=y_codes[1][:, a - HALF : b - HALF].bitcast(E4M3),
+                scales=y_scales[:, a:b],
+                in_=y_bf[1][:, a - HALF : b - HALF, :].rearrange("p n t -> p (n t)"),
             )
-            nc.sync.dma_start(words_out[:, halves[h]], y_codes[h][:].bitcast(I32))
+        nc.sync.dma_start(words_out[:, HALF:N], y_codes[1][:].bitcast(I32))
+        nc.vector.quantize_mx(
+            out=y_codes[0][:].bitcast(E4M3),
+            scales=y_scales[:, 0:HALF],
+            in_=y_bf[0][:].rearrange("p n t -> p (n t)"),
+        )
+        nc.sync.dma_start(words_out[:, 0:HALF], y_codes[0][:].bitcast(I32))
         for q in range(4):
             queue = nc.scalar if q < 2 else nc.sync
             queue.dma_start(scales_out[4 * q : 4 * q + 4, :], y_scales[32 * q : 32 * q + 4, :].bitcast(I32))

from contextlib import ExitStack

import concourse.mybir as mybir
from concourse.masks import make_identity

K, N, T, J = 512, 512, 2048, 512
FLOPS = 2 * K * N * J

F32 = mybir.dt.float32
BF16 = mybir.dt.bfloat16
I32 = mybir.dt.int32
U32 = mybir.dt.uint32
U16 = mybir.dt.uint16
U8 = mybir.dt.uint8
E4M3 = mybir.dt.float8_e4m3fn_x4
E5M2 = mybir.dt.float8_e5m2_x4
MULT = mybir.AluOpType.mult
ADD = mybir.AluOpType.add
COPY = mybir.ActivationFunctionType.Copy

P = 128
PACK = 4
HALF = N // 2
QUARTER = N // 4


def tile_list_wgrad_listed_pl_kernel(tc, xt, g, mom, offs, out_0, out_1, out_2):
    nc = tc.nc
    with ExitStack() as ctx:
        keep = ctx.enter_context(tc.tile_pool(name="keep", bufs=1))
        turn = ctx.enter_context(tc.psum_pool(name="turn", bufs=2))
        sums = ctx.enter_context(tc.psum_pool(name="sums", bufs=1))

        x_rows = xt.rearrange("(p t) c -> p (t c)", t=PACK)
        mom_rows = mom.rearrange("(p t) n -> p (t n)", t=PACK)
        y_rows = out_0.rearrange("(p t) n -> p (t n)", t=PACK)
        words_out = out_1.rearrange("z p c r -> p (z c r)").bitcast(I32)
        scales_out = out_2.rearrange("z q c -> (z q) c").bitcast(I32)

        offsets = keep.tile([P, J // 16], U16, name="offsets")
        g_win = [keep.tile([P, 2 * T], F32, name=f"g_win{c}") for c in range(2)]
        x_win = [keep.tile([P, T], F32, name=f"x_win{t}", tag=f"x_win{t}", align_bytes=64) for t in range(PACK)]
        mom01 = keep.tile([P, 2 * N], F32, name="mom01")
        mom23 = keep.tile([P, 2 * N], F32, name="mom23")

        g_rows = g.rearrange("(c p e) t -> c p (e t)", c=2, e=2)
        nc.sync.dma_start(g_win[0][:], g_rows[0])
        nc.sync.dma_start(offsets[:], offs)
        nc.sync.dma_start(g_win[1][:], g_rows[1])
        for t in range(PACK):
            nc.sync.dma_start(x_win[t][:], x_rows[:, t * T : (t + 1) * T])
        nc.sync.dma_start(mom01[:], mom_rows[:, 0 : 2 * N])
        nc.sync.dma_start(mom23[:], mom_rows[:, 2 * N : 4 * N])

        ident = keep.tile([P, P], F32, name="ident")
        make_identity(nc, ident[:])

        def listed_rows(windows, grouped, label):
            rows = len(windows)
            turned = turn.tile([P, rows, 2, P], F32, name="turned", tag="turned")
            for e, window in enumerate(windows):
                picked = keep.tile([P, J], BF16, name=f"picked_{label}_{e}", align_bytes=64)
                nc.vector.tensor_copy(
                    picked[:].rearrange("p (h b i) -> p b h i", h=2, i=16), window.indirect(offsets[:])
                )
                pairs = picked[:].bitcast(F32)
                for u in range(2):
                    nc.tensor.transpose(turned[:, e, u, :], pairs[:, u * P : (u + 1) * P], ident[:])
            nc.scalar.copy(
                grouped.bitcast(F32).rearrange("p (r e u) -> p r e u", e=rows, u=2),
                turned[:].rearrange("p e u r -> p r e u"),
            )

        g_grouped = keep.tile([P, N * PACK], BF16, name="g_grouped", align_bytes=64)
        for c in range(2):
            windows = [g_win[c][:, e * T : (e + 1) * T] for e in range(2)]
            listed_rows(windows, g_grouped[:, c * HALF * PACK : (c + 1) * HALF * PACK], f"g{c}")

        def regroup(t):
            x_grouped = keep.tile([P, P * PACK], BF16, name=f"x_grouped{t}", tag=f"x_grouped{t}", align_bytes=64)
            listed_rows([x_win[t][:]], x_grouped[:], f"x{t}")
            return x_grouped

        def product(t, x_grouped, codes_tag):
            x_codes = keep.tile([P, P], U32, name=f"x_codes{t}", tag=codes_tag, align_bytes=64)
            x_scales = keep.tile([P, P], U8, name=f"x_scales{t}", align_bytes=64)
            nc.vector.quantize_mx(out=x_codes[:].bitcast(E4M3), scales=x_scales[:], in_=x_grouped[:])
            w = sums.tile([P, N], F32, name=f"w{t}")
            nc.tensor.matmul_mx(
                out=w[:],
                lhsT=x_codes[:].bitcast(E4M3),
                lhsT_scale=x_scales[:],
                rhs=g_codes[:].bitcast(E5M2),
                rhs_scale=g_scales[:],
                start=True,
                stop=True,
            )
            return w

        def combine(y, w, kept):
            nc.vector.scalar_tensor_tensor(out=y, in0=w, scalar=0.04, in1=kept, op0=MULT, op1=ADD)

        grouped = [regroup(0)]
        g_codes = keep.tile([P, N], U32, name="g_codes", tag="x_win0", align_bytes=64)
        g_scales = keep.tile([P, N], U8, name="g_scales", align_bytes=64)
        nc.vector.quantize_mx(out=g_codes[:].bitcast(E5M2), scales=g_scales[:], in_=g_grouped[:])

        step = [keep.tile([P, N], F32, name=f"step{t}", tag=f"step{t}", align_bytes=64) for t in range(2)]
        for t in range(2):
            grouped.append(regroup(t + 1))
            w = product(t, grouped[t], f"x_win{t + 1}")
            nc.scalar.activation(step[t][:], w[:], COPY, scale=0.04)
        grouped.append(regroup(3))
        w2 = product(2, grouped[2], "x_win3")

        y01 = keep.tile([P, 2 * N], F32, name="y01")
        for t in range(2):
            cols = slice(t * N, (t + 1) * N)
            nc.vector.scalar_tensor_tensor(
                out=y01[:, cols], in0=mom01[:, cols], scalar=0.9, in1=step[t][:], op0=MULT, op1=ADD
            )
        nc.sync.dma_start(y_rows[:, 0 : 2 * N], y01[:])
        w3 = product(3, grouped[3], "step0")

        kept23 = keep.tile([P, 2 * N], F32, name="kept23")
        for t in range(2):
            cols = slice(t * N, (t + 1) * N)
            nc.scalar.activation(kept23[:, cols], mom23[:, cols], COPY, scale=0.9)

        y_bf = [
            keep.tile([P, HALF, PACK], BF16, name="y_bf0", tag="x_grouped3", align_bytes=64),
            keep.tile([P, HALF, PACK], BF16, name="y_bf1", align_bytes=64),
        ]
        y01_nt = y01[:].rearrange("p (t n) -> p n t", t=2)
        nc.scalar.copy(y_bf[0][:, :, 0:2], y01_nt[:, 0:HALF, :])
        nc.vector.tensor_copy(y_bf[1][:, :, 0:2], y01_nt[:, HALF:N, :])

        y23 = keep.tile([P, 2 * N], F32, name="y23")
        combine(y23[:, 0:N], w2[:], kept23[:, 0:N])
        nc.sync.dma_start(y_rows[:, 2 * N : 3 * N], y23[:, 0:N])
        quarters = [(HALF, HALF + QUARTER), (HALF + QUARTER, N)]
        for a, b in [(0, HALF)] + quarters:
            combine(y23[:, N + a : N + b], w3[:, a:b], kept23[:, N + a : N + b])
        nc.sync.dma_start(y_rows[:, 3 * N : 4 * N], y23[:, N : 2 * N])

        y23_nt = y23[:].rearrange("p (t n) -> p n t", t=2)
        nc.scalar.copy(y_bf[0][:, :, 2:4], y23_nt[:, 0:HALF, :])
        for a, b in quarters:
            nc.vector.tensor_copy(y_bf[1][:, a - HALF : b - HALF, 2:4], y23_nt[:, a:b, :])

        y_codes = [keep.tile([P, HALF], U32, name=f"y_codes{h}", align_bytes=64) for h in range(2)]
        y_scales = keep.tile([P, N], U8, name="y_scales", align_bytes=64)
        for a, b in quarters:
            nc.vector.quantize_mx(
                out=y_codes[1][:, a - HALF : b - HALF].bitcast(E4M3),
                scales=y_scales[:, a:b],
                in_=y_bf[1][:, a - HALF : b - HALF, :].rearrange("p n t -> p (n t)"),
            )
        nc.sync.dma_start(words_out[:, HALF:N], y_codes[1][:].bitcast(I32))
        nc.vector.quantize_mx(
            out=y_codes[0][:].bitcast(E4M3),
            scales=y_scales[:, 0:HALF],
            in_=y_bf[0][:].rearrange("p n t -> p (n t)"),
        )
        nc.sync.dma_start(words_out[:, 0:HALF], y_codes[0][:].bitcast(I32))
        for q in range(4):
            queue = nc.scalar if q < 2 else nc.sync
            queue.dma_start(scales_out[4 * q : 4 * q + 4, :], y_scales[32 * q : 32 * q + 4, :].bitcast(I32))
